import numpy as np, ml_dtypes
CORES = [34,35,38,39,42,43,46,47,162,163,166,167]
N = 12
ROOT = 5
WIDTHS = [256,51,0,0,512,256,256,256,256,0,512,512]
OFF = [0,256,307,307,307,819,1075,1331,1587,1843,1843,2355]
C = 2867
def setup_inputs(rng):
    return {"x": rng.standard_normal((N, 128, C), dtype=np.float32).astype(ml_dtypes.bfloat16)}
def reference(x):
    YW = max(WIDTHS)
    y = np.full((N, 128, YW), np.nan, x.dtype)
    for r in range(N):
        y[r][:, :WIDTHS[r]] = x[ROOT][:, OFF[r]:OFF[r] + WIDTHS[r]]
    return {"y": y}

@@ -1,0 +1,33 @@
+SCRATCH = {
+    "stage": ("sbuf", [128, 2867], "bfloat16"),
+}
+SEMAPHORES = ["own", "sent", "arrived", "stored"] + ["ld%d" % r for r in range(12)]
+
+
+def rank_program(g, core, T, topo):
+    rank = T.rank_of(core)
+    if rank is None:
+        return
+    W, OFF = T.tables["WIDTHS"], T.tables["OFF"]
+    root = T.cores[T.root]
+    if core == root:
+        g.scalar.dma_start(T.y[:, 0:W[rank]], T.x[:, OFF[rank]:OFF[rank] + W[rank]]).then_inc(T.sem.own, 16)
+        order = [r for r in range(12) if r != rank and W[r] > 0]
+        for r in order:
+            g.sync.dma_start(T.stage[:, OFF[r]:OFF[r] + W[r]], T.x[:, OFF[r]:OFF[r] + W[r]]).then_inc(T.sem["ld%d" % r], 16)
+        total = 0
+        for r in order:
+            d = T.cores[r]
+            rid, pid = topo.addr(d, core)
+            m = topo.mask(core, d)
+            n = 16 if m == 0xFFFF else 8
+            g.wait_ge(T.sem["ld%d" % r], 16)
+            g.remote_dma(T.stage[:, 0:W[r]], T.stage[:, OFF[r]:OFF[r] + W[r]], T.sem.arrived, T.sem.sent, pid, rid, m)
+            total += n
+        g.wait_ge(T.sem.sent, total)
+        g.wait_ge(T.sem.own, 16)
+    elif W[rank] > 0:
+        n = 16 if topo.mask(root, core) == 0xFFFF else 8
+        g.sync.wait_ge(T.sem.arrived, n)
+        g.sync.dma_start(T.y[:, 0:W[rank]], T.stage[:, 0:W[rank]]).then_inc(T.sem.stored, 16)
+        g.sync.wait_ge(T.sem.stored, 16)

@@ -1,33 +1,66 @@
-SCRATCH = {
-    "stage": ("sbuf", [128, 2867], "bfloat16"),
-}
-SEMAPHORES = ["own", "sent", "arrived", "stored"] + ["ld%d" % r for r in range(12)]
+ROOT_CORE = 43
+PIECE_W = [256, 51, 0, 0, 512, 256, 256, 256, 256, 0, 512, 512]
+
+FRAGS = [
+    ("fe2", 11, 58, 128, [45, 175]),
+    ("fd2", 10, 99, 128, [44, 174]),
+    ("fe1", 11, 0, 58, [171]),
+    ("fc2", 8, 45, 128, [170]),
+    ("fd0", 10, 0, 50, [46]),
+    ("fd1", 10, 50, 99, [47]),
+    ("fc1", 8, 0, 45, []),
+    ("fa", 0, 0, 128, []),
+    ("fb", 1, 0, 128, []),
+    ("ff", 4, 0, 128, []),
+    ("fg", 6, 0, 128, []),
+    ("fh", 7, 0, 128, []),
+]
+
+SCRATCH = {name: ("dram", [128, (p1 - p0) * PIECE_W[r] // 128], "bfloat16") for name, r, p0, p1, route in FRAGS}
+SEMAPHORES = [f[0] for f in FRAGS] + ["sent", "stored"]
+
+OFF_CHIP_ENGINES = 0x00FF
+ON_CHIP_ENGINES = 0xFF00
+N_ENG = 8
 
 
 def rank_program(g, core, T, topo):
-    rank = T.rank_of(core)
-    if rank is None:
-        return
     W, OFF = T.tables["WIDTHS"], T.tables["OFF"]
-    root = T.cores[T.root]
-    if core == root:
-        g.scalar.dma_start(T.y[:, 0:W[rank]], T.x[:, OFF[rank]:OFF[rank] + W[rank]]).then_inc(T.sem.own, 16)
-        order = [r for r in range(12) if r != rank and W[r] > 0]
-        for r in order:
-            g.sync.dma_start(T.stage[:, OFF[r]:OFF[r] + W[r]], T.x[:, OFF[r]:OFF[r] + W[r]]).then_inc(T.sem["ld%d" % r], 16)
-        total = 0
-        for r in order:
-            d = T.cores[r]
-            rid, pid = topo.addr(d, core)
-            m = topo.mask(core, d)
-            n = 16 if m == 0xFFFF else 8
-            g.wait_ge(T.sem["ld%d" % r], 16)
-            g.remote_dma(T.stage[:, 0:W[r]], T.stage[:, OFF[r]:OFF[r] + W[r]], T.sem.arrived, T.sem.sent, pid, rid, m)
-            total += n
-        g.wait_ge(T.sem.sent, total)
-        g.wait_ge(T.sem.own, 16)
-    elif W[rank] > 0:
-        n = 16 if topo.mask(root, core) == 0xFFFF else 8
-        g.sync.wait_ge(T.sem.arrived, n)
-        g.sync.dma_start(T.y[:, 0:W[rank]], T.stage[:, 0:W[rank]]).then_inc(T.sem.stored, 16)
-        g.sync.wait_ge(T.sem.stored, 16)
+    queues = [g.sync, g.scalar]
+    sent = 0
+    stored = 0
+
+    def send(name, dst):
+        rid, pid = topo.addr(dst, core)
+        on_chip = topo.mask(core, dst) == 0xFFFF
+        g.remote_dma(T[name][:], T[name][:], T.sem[name], T.sem.sent, pid, rid,
+                     ON_CHIP_ENGINES if on_chip else OFF_CHIP_ENGINES)
+
+    if core == ROOT_CORE:
+        for i, (name, r, p0, p1, route) in enumerate(FRAGS):
+            queues[i % 2].dma_start(T[name][:], T.x[p0:p1, OFF[r]:OFF[r] + W[r]]).then_inc(T.sem[name], 16)
+        r = T.root
+        g.sync.dma_start(T.y[:, 0:W[r]], T.x[:, OFF[r]:OFF[r] + W[r]]).then_inc(T.sem.stored, 16)
+        stored += 16
+        for name, r, p0, p1, route in FRAGS:
+            g.wait_ge(T.sem[name], 16)
+            send(name, (route + [T.cores[r]])[0])
+            sent += N_ENG
+    else:
+        for name, r, p0, p1, route in FRAGS:
+            if core in route:
+                g.wait_ge(T.sem[name], N_ENG)
+                send(name, (route + [T.cores[r]])[route.index(core) + 1])
+                sent += N_ENG
+        mine = [f for f in FRAGS if T.cores[f[1]] == core]
+        mine.sort(key=lambda f: len(f[4]))
+        for i, (name, r, p0, p1, route) in enumerate(mine):
+            q = queues[i % 2]
+            q.wait_ge(T.sem[name], N_ENG)
+            q.dma_start(T.y[p0:p1, 0:W[r]], T[name][:]).then_inc(T.sem.stored, 16)
+            stored += 16
+
+    if sent:
+        g.wait_ge(T.sem.sent, sent)
+    if stored:
+        g.wait_ge(T.sem.stored, stored)

ROOT_CORE = 43
PIECE_W = [256, 51, 0, 0, 512, 256, 256, 256, 256, 0, 512, 512]

FRAGS = [
    ("fe2", 11, 58, 128, [45, 175]),
    ("fd2", 10, 99, 128, [44, 174]),
    ("fe1", 11, 0, 58, [171]),
    ("fc2", 8, 45, 128, [170]),
    ("fd0", 10, 0, 50, [46]),
    ("fd1", 10, 50, 99, [47]),
    ("fc1", 8, 0, 45, []),
    ("fa", 0, 0, 128, []),
    ("fb", 1, 0, 128, []),
    ("ff", 4, 0, 128, []),
    ("fg", 6, 0, 128, []),
    ("fh", 7, 0, 128, []),
]

SCRATCH = {name: ("dram", [128, (p1 - p0) * PIECE_W[r] // 128], "bfloat16") for name, r, p0, p1, route in FRAGS}
SEMAPHORES = [f[0] for f in FRAGS] + ["sent", "stored"]

OFF_CHIP_ENGINES = 0x00FF
ON_CHIP_ENGINES = 0xFF00
N_ENG = 8


def rank_program(g, core, T, topo):
    W, OFF = T.tables["WIDTHS"], T.tables["OFF"]
    queues = [g.sync, g.scalar]
    sent = 0
    stored = 0

    def send(name, dst):
        rid, pid = topo.addr(dst, core)
        on_chip = topo.mask(core, dst) == 0xFFFF
        g.remote_dma(T[name][:], T[name][:], T.sem[name], T.sem.sent, pid, rid,
                     ON_CHIP_ENGINES if on_chip else OFF_CHIP_ENGINES)

    if core == ROOT_CORE:
        for i, (name, r, p0, p1, route) in enumerate(FRAGS):
            queues[i % 2].dma_start(T[name][:], T.x[p0:p1, OFF[r]:OFF[r] + W[r]]).then_inc(T.sem[name], 16)
        r = T.root
        g.sync.dma_start(T.y[:, 0:W[r]], T.x[:, OFF[r]:OFF[r] + W[r]]).then_inc(T.sem.stored, 16)
        stored += 16
        for name, r, p0, p1, route in FRAGS:
            g.wait_ge(T.sem[name], 16)
            send(name, (route + [T.cores[r]])[0])
            sent += N_ENG
    else:
        for name, r, p0, p1, route in FRAGS:
            if core in route:
                g.wait_ge(T.sem[name], N_ENG)
                send(name, (route + [T.cores[r]])[route.index(core) + 1])
                sent += N_ENG
        mine = [f for f in FRAGS if T.cores[f[1]] == core]
        mine.sort(key=lambda f: len(f[4]))
        for i, (name, r, p0, p1, route) in enumerate(mine):
            q = queues[i % 2]
            q.wait_ge(T.sem[name], N_ENG)
            q.dma_start(T.y[p0:p1, 0:W[r]], T[name][:]).then_inc(T.sem.stored, 16)
            stored += 16

    if sent:
        g.wait_ge(T.sem.sent, sent)
    if stored:
        g.wait_ge(T.sem.stored, stored)
